import numpy as np
import ml_dtypes

BF16 = ml_dtypes.bfloat16


def bf(x):
    return np.asarray(x, np.float32).astype(BF16)


def f32(x):
    return np.asarray(x, np.float32)


def f64(x):
    return np.asarray(x).astype(np.float64)


def striped(idx):
    return np.tile(idx.reshape(-1, 16).T, (8, 1))


S, K, M, N, E, Q, O = 512, 128, 256, 192, 2, 96, 128


def gelu_tanh(v):
    return 0.5 * v * (1.0 + np.tanh(np.sqrt(2.0 / np.pi) * (v + 0.044715 * v**3)))


def setup_inputs():
    return {"base": bf(np.random.standard_normal((M, S))), "x": bf(np.random.standard_normal((K, N))), "w": bf(1.2 * np.random.standard_normal((E, K, M)) / np.sqrt(K)), "w2": bf(np.random.standard_normal((M, O)) / np.sqrt(2 * M)), "b": f32(0.5 * np.random.standard_normal((O, 1))), "offs": striped(np.random.permutation(S)[:N])}


def reference(base, x, w, w2, b, offs):
    idx = offs[:16].T.reshape(-1)
    z = f64(base).copy()
    for e in range(E):
        z[:, idx[e * Q : (e + 1) * Q]] += f64(w)[e].T @ f64(x)[:, e * Q : (e + 1) * Q]
    y = f64(w2).T @ z
    return gelu_tanh(y + f64(b))

@@ -1,0 +1,66 @@
+import concourse.mybir as mybir
+from concourse.masks import make_identity
+
+BF16, F32, U16 = mybir.dt.bfloat16, mybir.dt.float32, mybir.dt.uint16
+GELU = mybir.ActivationFunctionType.Gelu_apprx_tanh
+
+P = 128
+TOKENS, FEATURES, OUT_FEATURES = 512, 256, 128
+EXPERTS, ENTRIES = 2, 192
+PIECE = ENTRIES // EXPERTS
+BLOCKS = FEATURES // P
+
+FLOPS = 2 * P * FEATURES * ENTRIES + 2 * FEATURES * OUT_FEATURES * TOKENS
+
+
+def tile_rows_thenproj_gelu_kernel(tc, base, x, w, w2, b, offs, out):
+    nc = tc.nc
+    with (
+        tc.tile_pool(name="held", bufs=1) as held,
+        tc.psum_pool(name="psum", bufs=1) as psum,
+    ):
+        offsets = held.tile([P, ENTRIES // 16], U16)
+        base_sb = held.tile([P, BLOCKS, TOKENS], BF16)
+        w_sb = held.tile([P, EXPERTS, FEATURES], BF16)
+        x_sb = held.tile([P, ENTRIES], BF16)
+        w2_sb = held.tile([P, BLOCKS, OUT_FEATURES], BF16)
+        bias = held.tile([P, 1], F32)
+        nc.sync.dma_start(base_sb[:], base.rearrange("(a p) s -> p a s", p=P))
+        nc.sync.dma_start(offsets[:], offs)
+        nc.scalar.dma_start(w_sb[:], w.rearrange("e k m -> k e m"))
+        nc.scalar.dma_start(x_sb[:], x)
+        nc.scalar.dma_start(w2_sb[:], w2.rearrange("(a p) o -> p a o", p=P))
+        nc.scalar.dma_start(bias[:], b)
+
+        early = held.tile([P, 1], F32)
+        nc.vector.memset(early[:], 0.0)
+        nc.scalar.activation(early[:], early[:], GELU)
+
+        ident = held.tile([P, P], BF16)
+        make_identity(nc, ident[:])
+
+        windows = [psum.tile([P, TOKENS], F32, name=f"window{a}") for a in range(BLOCKS)]
+        for a in range(BLOCKS):
+            nc.tensor.matmul(windows[a][:], ident[:], base_sb[:, a, :], start=True, stop=False)
+
+        cols = PIECE // 16
+        for a in range(BLOCKS):
+            for e in range(EXPERTS):
+                nc.tensor.matmul(
+                    windows[a][:].indirect(offsets[:, e * cols : (e + 1) * cols]),
+                    w_sb[:, e, a * P : (a + 1) * P],
+                    x_sb[:, e * PIECE : (e + 1) * PIECE],
+                    start=False,
+                    stop=e == EXPERTS - 1,
+                )
+
+        z = [held.tile([P, TOKENS], BF16, name=f"z{a}") for a in range(BLOCKS)]
+        nc.vector.tensor_copy(z[0][:], windows[0][:])
+        nc.scalar.copy(z[1][:], windows[1][:])
+
+        y = psum.tile([P, TOKENS], F32)
+        for a in range(BLOCKS):
+            nc.tensor.matmul(y[:], w2_sb[:, a, :], z[a][:], start=a == 0, stop=a == BLOCKS - 1)
+        out_sb = held.tile([P, TOKENS], F32)
+        nc.scalar.activation(out_sb[:], y[:], GELU, bias=bias[:])
+        nc.sync.dma_start(out, out_sb[:])

@@ -36,6 +36,12 @@ def tile_rows_thenproj_gelu_kernel(tc, base, x, w, w2, b, offs, out):
         nc.vector.memset(early[:], 0.0)
         nc.scalar.activation(early[:], early[:], GELU)
 
+        zeros = held.tile([P, TOKENS], BF16)
+        nc.vector.memset(zeros[:], 0.0)
+        spare = psum.tile([P, TOKENS], F32)
+        for turn in range(4):
+            nc.tensor.matmul(spare[:], zeros[:, 0:P], zeros[:], start=True, stop=True)
+
         ident = held.tile([P, P], BF16)
         make_identity(nc, ident[:])
 
@@ -54,13 +60,18 @@ def tile_rows_thenproj_gelu_kernel(tc, base, x, w, w2, b, offs, out):
                     stop=e == EXPERTS - 1,
                 )
 
+        HALF = TOKENS // 2
         z = [held.tile([P, TOKENS], BF16, name=f"z{a}") for a in range(BLOCKS)]
-        nc.vector.tensor_copy(z[0][:], windows[0][:])
-        nc.scalar.copy(z[1][:], windows[1][:])
+        for h in range(2):
+            half = slice(h * HALF, (h + 1) * HALF)
+            nc.vector.tensor_copy(z[0][:, half], windows[0][:, half])
+            nc.scalar.copy(z[1][:, half], windows[1][:, half])
 
-        y = psum.tile([P, TOKENS], F32)
-        for a in range(BLOCKS):
-            nc.tensor.matmul(y[:], w2_sb[:, a, :], z[a][:], start=a == 0, stop=a == BLOCKS - 1)
-        out_sb = held.tile([P, TOKENS], F32)
-        nc.scalar.activation(out_sb[:], y[:], GELU, bias=bias[:])
-        nc.sync.dma_start(out, out_sb[:])
+        for h in range(2):
+            half = slice(h * HALF, (h + 1) * HALF)
+            y = psum.tile([P, HALF], F32, name=f"y{h}")
+            for a in range(BLOCKS):
+                nc.tensor.matmul(y[:], w2_sb[:, a, :], z[a][:, half], start=a == 0, stop=a == BLOCKS - 1)
+            out_sb = held.tile([P, HALF], F32, name=f"out{h}")
+            nc.scalar.activation(out_sb[:], y[:], GELU, bias=bias[:])
+            nc.sync.dma_start(out[:, half], out_sb[:])

@@ -27,10 +27,10 @@ def tile_rows_thenproj_gelu_kernel(tc, base, x, w, w2, b, offs, out):
         bias = held.tile([P, 1], F32)
         nc.sync.dma_start(base_sb[:], base.rearrange("(a p) s -> p a s", p=P))
         nc.sync.dma_start(offsets[:], offs)
-        nc.scalar.dma_start(w_sb[:], w.rearrange("e k m -> k e m"))
-        nc.scalar.dma_start(x_sb[:], x)
-        nc.scalar.dma_start(w2_sb[:], w2.rearrange("(a p) o -> p a o", p=P))
-        nc.scalar.dma_start(bias[:], b)
+        nc.sync.dma_start(w_sb[:], w.rearrange("e k m -> k e m"))
+        nc.sync.dma_start(x_sb[:], x)
+        nc.sync.dma_start(w2_sb[:], w2.rearrange("(a p) o -> p a o", p=P))
+        nc.sync.dma_start(bias[:], b)
 
         early = held.tile([P, 1], F32)
         nc.vector.memset(early[:], 0.0)

import concourse.mybir as mybir
from concourse.masks import make_identity

BF16, F32, U16 = mybir.dt.bfloat16, mybir.dt.float32, mybir.dt.uint16
GELU = mybir.ActivationFunctionType.Gelu_apprx_tanh

P = 128
TOKENS, FEATURES, OUT_FEATURES = 512, 256, 128
EXPERTS, ENTRIES = 2, 192
PIECE = ENTRIES // EXPERTS
BLOCKS = FEATURES // P

FLOPS = 2 * P * FEATURES * ENTRIES + 2 * FEATURES * OUT_FEATURES * TOKENS


def tile_rows_thenproj_gelu_kernel(tc, base, x, w, w2, b, offs, out):
    nc = tc.nc
    with (
        tc.tile_pool(name="held", bufs=1) as held,
        tc.psum_pool(name="psum", bufs=1) as psum,
    ):
        offsets = held.tile([P, ENTRIES // 16], U16)
        base_sb = held.tile([P, BLOCKS, TOKENS], BF16)
        w_sb = held.tile([P, EXPERTS, FEATURES], BF16)
        x_sb = held.tile([P, ENTRIES], BF16)
        w2_sb = held.tile([P, BLOCKS, OUT_FEATURES], BF16)
        bias = held.tile([P, 1], F32)
        nc.sync.dma_start(base_sb[:], base.rearrange("(a p) s -> p a s", p=P))
        nc.sync.dma_start(offsets[:], offs)
        nc.sync.dma_start(w_sb[:], w.rearrange("e k m -> k e m"))
        nc.sync.dma_start(x_sb[:], x)
        nc.sync.dma_start(w2_sb[:], w2.rearrange("(a p) o -> p a o", p=P))
        nc.sync.dma_start(bias[:], b)

        early = held.tile([P, 1], F32)
        nc.vector.memset(early[:], 0.0)
        nc.scalar.activation(early[:], early[:], GELU)

        zeros = held.tile([P, TOKENS], BF16)
        nc.vector.memset(zeros[:], 0.0)
        spare = psum.tile([P, TOKENS], F32)
        for turn in range(4):
            nc.tensor.matmul(spare[:], zeros[:, 0:P], zeros[:], start=True, stop=True)

        ident = held.tile([P, P], BF16)
        make_identity(nc, ident[:])

        windows = [psum.tile([P, TOKENS], F32, name=f"window{a}") for a in range(BLOCKS)]
        for a in range(BLOCKS):
            nc.tensor.matmul(windows[a][:], ident[:], base_sb[:, a, :], start=True, stop=False)

        cols = PIECE // 16
        for a in range(BLOCKS):
            for e in range(EXPERTS):
                nc.tensor.matmul(
                    windows[a][:].indirect(offsets[:, e * cols : (e + 1) * cols]),
                    w_sb[:, e, a * P : (a + 1) * P],
                    x_sb[:, e * PIECE : (e + 1) * PIECE],
                    start=False,
                    stop=e == EXPERTS - 1,
                )

        HALF = TOKENS // 2
        z = [held.tile([P, TOKENS], BF16, name=f"z{a}") for a in range(BLOCKS)]
        for h in range(2):
            half = slice(h * HALF, (h + 1) * HALF)
            nc.vector.tensor_copy(z[0][:, half], windows[0][:, half])
            nc.scalar.copy(z[1][:, half], windows[1][:, half])

        for h in range(2):
            half = slice(h * HALF, (h + 1) * HALF)
            y = psum.tile([P, HALF], F32, name=f"y{h}")
            for a in range(BLOCKS):
                nc.tensor.matmul(y[:], w2_sb[:, a, :], z[a][:, half], start=a == 0, stop=a == BLOCKS - 1)
            out_sb = held.tile([P, HALF], F32, name=f"out{h}")
            nc.scalar.activation(out_sb[:], y[:], GELU, bias=bias[:])
            nc.sync.dma_start(out[:, half], out_sb[:])
